import numpy as np
import ml_dtypes


def mxq(x, axis, fmt="e4m3"):
    dtype, down = {"e4m3": (ml_dtypes.float8_e4m3fn, 7), "e5m2": (ml_dtypes.float8_e5m2, 14)}[fmt]
    v = np.moveaxis(np.asarray(x, np.float32).astype(ml_dtypes.bfloat16).astype(np.float64), axis, -1)
    blocks = v.reshape(v.shape[:-1] + (-1, 32))
    amax = np.abs(blocks).max(-1, keepdims=True)
    byte = np.maximum(np.where(amax > 0, np.frexp(amax)[1] - 1 + 127, 0) - down, 1)
    scale = np.exp2(byte - 127.0)
    codes = (blocks / scale).astype(np.float32).astype(dtype).astype(np.float64)
    return np.moveaxis((codes * scale).reshape(v.shape), -1, axis)


WIDE = False


def mx_kscale(k):
    if not WIDE:
        return np.ones(k)
    levels = np.array([10, -10, 5, -5, 0])
    if k % 512:
        return np.exp2(np.random.permutation(np.resize(levels, k // 32))).repeat(32)
    a = np.empty((k // 512, 16))
    for p in range(k // 512):
        a[p, :8] = np.random.permutation(np.resize(levels, 8))
        for g in range(8):
            far = levels[np.abs(levels - a[p, g]) >= 10]
            a[p, g + 8] = far[np.random.randint(len(far))]
    return np.exp2(a.ravel()).repeat(32)


def f64(x):
    return np.asarray(x).astype(np.float64)


def striped(idx):
    return np.tile(idx.reshape(-1, 16).T, (8, 1)).astype(np.uint16)


def unstriped(offs):
    return offs[:16].T.reshape(-1).astype(np.int64)


def pack_weight(w):
    k, n = w.shape
    w = f64(np.asarray(w, np.float32).astype(ml_dtypes.bfloat16)).reshape(k // 32, 32, n)
    amax = np.abs(w).max(1)
    byte = np.clip(np.where(amax > 0, np.frexp(amax)[1] - 1 + 127 - 7, 1), 1, 254)
    scaled = (w * np.exp2(127.0 - byte)[:, None, :]).reshape(k, n).astype(np.float32)
    words = np.ascontiguousarray(scaled.reshape(k // 512, 128, 4, n).transpose(0, 1, 3, 2)).astype(ml_dtypes.float8_e4m3fn).view(np.uint8)
    return words, np.ascontiguousarray(byte.astype(np.uint8).reshape(k // 512, 16, n))


def unpack_weight(words, scales):
    g, p, n, _ = words.shape
    vals = np.ascontiguousarray(words).view(ml_dtypes.float8_e4m3fn).astype(np.float64) * np.repeat(np.exp2(scales.astype(np.float64) - 127.0), 8, axis=1)[..., None]
    return vals.transpose(0, 1, 3, 2).reshape(g * 512, n)


K, T, S, V = 1024, 1024, 512, 256


def setup_inputs():
    n = np.random.standard_normal
    s = mx_kscale(K)[:, None]
    packed_xT = pack_weight(n((K, T)) * s)
    return {
        "x_words": packed_xT[0],
        "x_scales": packed_xT[1],
        "hT": (n((K, V)) / np.sqrt(K) / s).astype(np.float32),
        "lib": (np.random.uniform(0.0, 1.0, (V, S)) ** 3 + 0.001).astype(np.float32),
        "offs": striped(np.random.permutation(T)[:S]),
    }


def reference(x_words, x_scales, hT, lib, offs):
    hTq = mxq(f64(hT), 0, "e4m3")
    xq = unpack_weight(x_words, x_scales)[:, unstriped(offs)]
    ea = np.exp(hTq.T @ xq)
    ta = ea.sum(axis=1, keepdims=True)
    pa = ea / ta
    tb = f64(lib).sum(axis=1, keepdims=True)
    pb = f64(lib) / tb
    mid = 0.5 * (pa + pb)
    return 300.0 * (pa * (np.log(500.0 * pa + 0.01) - np.log(500.0 * mid + 0.01)) + pb * (np.log(500.0 * pb + 0.01) - np.log(500.0 * mid + 0.01)))

@@ -1,0 +1,176 @@
+from contextlib import ExitStack
+
+import concourse.mybir as mybir
+
+K, T, S, V = 1024, 1024, 512, 256
+FLOPS = 2 * K * V * S
+
+F32 = mybir.dt.float32
+BF16 = mybir.dt.bfloat16
+I32 = mybir.dt.int32
+U32 = mybir.dt.uint32
+U16 = mybir.dt.uint16
+U8 = mybir.dt.uint8
+FP8X4 = mybir.dt.float8_e4m3fn_x4
+ALU = mybir.AluOpType
+ACT = mybir.ActivationFunctionType
+AX = mybir.AxisListType
+
+P = 128
+PACK = 4
+PASSES = K // (P * PACK)
+TILES = V // P
+
+
+def tile_picked_yspent_sim_p_kernel(tc, x_words, x_scales, hT, lib, offs, out):
+    nc = tc.nc
+    with ExitStack() as ctx:
+        keep = ctx.enter_context(tc.tile_pool(name="keep", bufs=1))
+        psum = ctx.enter_context(tc.psum_pool(name="psum", bufs=1))
+
+        def sb(name, shape, dtype):
+            return keep.tile(shape, dtype, name=name, align_bytes=64)
+
+        offsets = keep.tile([P, S // 16], U16, name="offsets")
+        nc.sync.dma_start(offsets[:], offs)
+
+        warm = sb("warm", [P, 2], F32)
+        nc.gpsimd.memset(warm[:, 0:1], 0.0)
+
+        x_planes = sb("x_planes", [P, T], U8)
+        nc.vector.memset(x_planes[:].bitcast(I32), 0)
+        for q in range(4):
+            nc.scalar.dma_start(
+                out=x_planes[32 * q : 32 * q + 4 * PASSES, :].bitcast(I32),
+                in_=x_scales[:, 4 * q : 4 * q + 4, :].bitcast(I32),
+            )
+        nc.scalar.activation(warm[:, 1:2], warm[:, 0:1], ACT.Exp)
+
+        x_table, h_raw = [], []
+        for o in range(PASSES):
+            xt = sb(f"x_table{o}", [P, T], I32)
+            nc.sync.dma_start(out=xt[:], in_=x_words[o].rearrange("p c r -> p (c r)").bitcast(I32))
+            x_table.append(xt)
+            hr = sb(f"h_raw{o}", [P, PACK, V], F32)
+            nc.sync.dma_start(out=hr[:], in_=hT[o * P * PACK : (o + 1) * P * PACK, :].rearrange("(p j) v -> p j v", j=PACK))
+            h_raw.append(hr)
+        lib_t = []
+        for m in range(TILES):
+            lt = sb(f"lib{m}", [P, S], F32)
+            nc.sync.dma_start(out=lt[:], in_=lib[m * P : (m + 1) * P, :])
+            lib_t.append(lt)
+
+        x_codes = [sb(f"x_codes{o}", [P, S], U32) for o in range(PASSES)]
+        x_sc = sb("x_sc", [P, S], U8)
+        h_bf = [[sb(f"h_bf{o}{m}", [P, P, PACK], BF16) for m in range(TILES)] for o in range(PASSES)]
+        h_codes = [[sb(f"h_codes{o}{m}", [P, P], U32) for m in range(TILES)] for o in range(PASSES)]
+        h_sc = [[sb(f"h_sc{o}{m}", [P, P], U8) for m in range(TILES)] for o in range(PASSES)]
+        z = [psum.tile([P, S], F32, name=f"z{m}") for m in range(TILES)]
+
+        def gather_words(o):
+            nc.vector.tensor_copy(x_codes[o][:], x_table[o][:].bitcast(U32).indirect(offsets[:]))
+
+        def weave(copy, o, m):
+            copy(
+                h_bf[o][m][:].rearrange("p (c i) j -> p c j i", i=4),
+                h_raw[o][:, :, m * P : (m + 1) * P].rearrange("p j (c i) -> p c j i", i=4),
+            )
+
+        def quantise(o, m):
+            nc.vector.quantize_mx(
+                out=h_codes[o][m][:].bitcast(FP8X4),
+                scales=h_sc[o][m][:],
+                in_=h_bf[o][m][:].rearrange("p c j -> p (c j)"),
+            )
+
+        def product(o, m):
+            nc.tensor.matmul_mx(
+                out=z[m][:],
+                lhsT=h_codes[o][m][:].bitcast(FP8X4),
+                lhsT_scale=h_sc[o][m][:],
+                rhs=x_codes[o][:].bitcast(FP8X4),
+                rhs_scale=x_sc[4 * o :, :],
+                start=(o == 0),
+                stop=(o == PASSES - 1),
+            )
+
+        gather_words(0)
+        nc.vector.tensor_copy(x_sc[:], x_planes[:].indirect(offsets[:]))
+        weave(nc.scalar.copy, 0, 0)
+        weave(nc.scalar.copy, 0, 1)
+        quantise(0, 0)
+        quantise(0, 1)
+        product(0, 0)
+        product(0, 1)
+        gather_words(1)
+        weave(nc.scalar.copy, 1, 0)
+        weave(nc.vector.tensor_copy, 1, 1)
+        quantise(1, 0)
+        quantise(1, 1)
+        product(1, 0)
+        product(1, 1)
+
+        neg_max = [sb(f"neg_max{m}", [P, 1], F32) for m in range(TILES)]
+        ta = [sb(f"ta{m}", [P, 1], F32) for m in range(TILES)]
+        ra = [sb(f"ra{m}", [P, 1], F32) for m in range(TILES)]
+        tb = sb("tb", [P, TILES], F32)
+        rb300 = sb("rb300", [P, TILES], F32)
+        rb500 = sb("rb500", [P, TILES], F32)
+        e = [sb(f"e{m}", [P, S], F32) for m in range(TILES)]
+        a = [sb(f"a{m}", [P, S], F32) for m in range(TILES)]
+        s = [sb(f"s{m}", [P, S], F32) for m in range(TILES)]
+        ln_a = [sb(f"ln_a{m}", [P, S], F32) for m in range(TILES)]
+        ln_m = [sb(f"ln_m{m}", [P, S], F32) for m in range(TILES)]
+        ln_b = [e[1], e[0]]
+        t_a = [sb(f"t_a{m}", [P, S], F32) for m in range(TILES)]
+        t_m = [sb(f"t_m{m}", [P, S], F32) for m in range(TILES)]
+        t_b = [sb(f"t_b{m}", [P, S], F32) for m in range(TILES)]
+        d = [sb(f"d{m}", [P, S], F32) for m in range(TILES)]
+        res = [sb(f"res{m}", [P, S], F32) for m in range(TILES)]
+
+        for m in range(TILES):
+            nc.scalar.activation(t_b[m][:], lib_t[m][:], ACT.Copy, scale=1.0 / 300.0, accum_out=tb[:, m : m + 1])
+        for m in range(TILES):
+            nc.vector.tensor_reduce(neg_max[m][:], z[m][:], AX.X, ALU.max, negate=True)
+            nc.scalar.activation(e[m][:], z[m][:], ACT.Exp, bias=neg_max[m][:], accum_out=ta[m][:])
+        nc.vector.reciprocal(rb300[:], tb[:])
+        nc.vector.reciprocal(ra[0][:], ta[0][:])
+        nc.vector.tensor_scalar(rb500[:], rb300[:], 500.0 / 300.0, None, ALU.mult)
+        nc.vector.tensor_scalar(a[0][:], e[0][:], ra[0][:], 300.0, ALU.mult, ALU.mult)
+        nc.vector.reciprocal(ra[1][:], ta[1][:])
+        nc.vector.scalar_tensor_tensor(s[0][:], lib_t[0][:], rb300[:, 0:1], a[0][:], ALU.mult, ALU.add)
+        nc.vector.tensor_scalar(a[1][:], e[1][:], ra[1][:], 300.0, ALU.mult, ALU.mult)
+        nc.vector.scalar_tensor_tensor(s[1][:], lib_t[1][:], rb300[:, 1:2], a[1][:], ALU.mult, ALU.add)
+
+        for m in range(TILES):
+            nc.scalar.activation(ln_a[m][:], a[m][:], ACT.Ln, scale=500.0 / 300.0, bias=0.01)
+            nc.scalar.activation(ln_m[m][:], s[m][:], ACT.Ln, scale=250.0 / 300.0, bias=0.01)
+            nc.scalar.activation(ln_b[m][:], lib_t[m][:], ACT.Ln, scale=rb500[:, m : m + 1], bias=0.01)
+
+        def term_a(m):
+            nc.vector.tensor_tensor(t_a[m][:], a[m][:], ln_a[m][:], ALU.mult)
+
+        def term_m(m):
+            nc.vector.tensor_tensor(t_m[m][:], s[m][:], ln_m[m][:], ALU.mult)
+
+        def term_b(m):
+            nc.vector.scalar_tensor_tensor(t_b[m][:], lib_t[m][:], rb300[:, m : m + 1], ln_b[m][:], ALU.mult, ALU.mult)
+
+        def diff(m):
+            nc.vector.tensor_tensor(d[m][:], t_a[m][:], t_m[m][:], ALU.subtract)
+
+        def finish(m, cols):
+            nc.vector.tensor_tensor(res[m][:, cols], d[m][:, cols], t_b[m][:, cols], ALU.add)
+            nc.sync.dma_start(out=out[m * P : (m + 1) * P, cols], in_=res[m][:, cols])
+
+        term_a(0)
+        term_m(0)
+        term_b(0)
+        diff(0)
+        term_a(1)
+        finish(0, slice(0, S))
+        term_m(1)
+        term_b(1)
+        diff(1)
+        finish(1, slice(0, S // 2))
+        finish(1, slice(S // 2, S))

@@ -1,6 +1,7 @@
 from contextlib import ExitStack
 
 import concourse.mybir as mybir
+from concourse.masks import make_identity
 
 K, T, S, V = 1024, 1024, 512, 256
 FLOPS = 2 * K * V * S
@@ -34,16 +35,12 @@ def tile_picked_yspent_sim_p_kernel(tc, x_words, x_scales, hT, lib, offs, out):
         offsets = keep.tile([P, S // 16], U16, name="offsets")
         nc.sync.dma_start(offsets[:], offs)
 
-        warm = sb("warm", [P, 2], F32)
-        nc.gpsimd.memset(warm[:, 0:1], 0.0)
-
         x_planes = sb("x_planes", [P, T], U8)
         nc.vector.memset(x_planes[:].bitcast(I32), 0)
-        for q in range(4):
-            nc.scalar.dma_start(
-                out=x_planes[32 * q : 32 * q + 4 * PASSES, :].bitcast(I32),
-                in_=x_scales[:, 4 * q : 4 * q + 4, :].bitcast(I32),
-            )
+        warm = sb("warm", [P, 2], F32)
+        nc.vector.memset(warm[:, 0:1], 0.0)
+        ident = sb("ident", [P, P], F32)
+        make_identity(nc, ident[:])
         nc.scalar.activation(warm[:, 1:2], warm[:, 0:1], ACT.Exp)
 
         x_table, h_raw = [], []
@@ -51,6 +48,12 @@ def tile_picked_yspent_sim_p_kernel(tc, x_words, x_scales, hT, lib, offs, out):
             xt = sb(f"x_table{o}", [P, T], I32)
             nc.sync.dma_start(out=xt[:], in_=x_words[o].rearrange("p c r -> p (c r)").bitcast(I32))
             x_table.append(xt)
+            if o == 0:
+                for q in range(4):
+                    nc.sync.dma_start(
+                        out=x_planes[32 * q : 32 * q + 4 * PASSES, :].bitcast(I32),
+                        in_=x_scales[:, 4 * q : 4 * q + 4, :].bitcast(I32),
+                    )
             hr = sb(f"h_raw{o}", [P, PACK, V], F32)
             nc.sync.dma_start(out=hr[:], in_=hT[o * P * PACK : (o + 1) * P * PACK, :].rearrange("(p j) v -> p j v", j=PACK))
             h_raw.append(hr)
@@ -114,63 +117,84 @@ def tile_picked_yspent_sim_p_kernel(tc, x_words, x_scales, hT, lib, offs, out):
         ta = [sb(f"ta{m}", [P, 1], F32) for m in range(TILES)]
         ra = [sb(f"ra{m}", [P, 1], F32) for m in range(TILES)]
         tb = sb("tb", [P, TILES], F32)
-        rb300 = sb("rb300", [P, TILES], F32)
-        rb500 = sb("rb500", [P, TILES], F32)
+        rb = sb("rb", [P, TILES], F32)
         e = [sb(f"e{m}", [P, S], F32) for m in range(TILES)]
         a = [sb(f"a{m}", [P, S], F32) for m in range(TILES)]
-        s = [sb(f"s{m}", [P, S], F32) for m in range(TILES)]
-        ln_a = [sb(f"ln_a{m}", [P, S], F32) for m in range(TILES)]
-        ln_m = [sb(f"ln_m{m}", [P, S], F32) for m in range(TILES)]
-        ln_b = [e[1], e[0]]
-        t_a = [sb(f"t_a{m}", [P, S], F32) for m in range(TILES)]
-        t_m = [sb(f"t_m{m}", [P, S], F32) for m in range(TILES)]
-        t_b = [sb(f"t_b{m}", [P, S], F32) for m in range(TILES)]
-        d = [sb(f"d{m}", [P, S], F32) for m in range(TILES)]
+        b = [sb(f"b{m}", [P, S], F32) for m in range(TILES)]
+        n = [sb(f"n{m}", [P, S], F32) for m in range(TILES)]
         res = [sb(f"res{m}", [P, S], F32) for m in range(TILES)]
 
         for m in range(TILES):
-            nc.scalar.activation(t_b[m][:], lib_t[m][:], ACT.Copy, scale=1.0 / 300.0, accum_out=tb[:, m : m + 1])
+            nc.scalar.activation(e[m][:], lib_t[m][:], ACT.Copy, scale=1.0 / 300.0, accum_out=tb[:, m : m + 1])
         for m in range(TILES):
             nc.vector.tensor_reduce(neg_max[m][:], z[m][:], AX.X, ALU.max, negate=True)
             nc.scalar.activation(e[m][:], z[m][:], ACT.Exp, bias=neg_max[m][:], accum_out=ta[m][:])
-        nc.vector.reciprocal(rb300[:], tb[:])
+        nc.vector.reciprocal(rb[:], tb[:])
+        def scale_b(m):
+            nc.vector.tensor_scalar(b[m][:], lib_t[m][:], rb[:, m : m + 1], None, ALU.mult)
+
+        def scale_a(m):
+            nc.vector.tensor_scalar(a[m][:], e[m][:], ra[m][:], 300.0, ALU.mult, ALU.mult)
+
+        def neg_sum(m):
+            nc.vector.tensor_tensor(n[m][:], a[m][:], b[m][:], ALU.add)
+
+        HALF = S // 2
+        units = [(m, h) for m in range(TILES) for h in range(2)]
+        turned = [psum.tile([P, S], F32, name=f"turned{u}") for u in range(len(units))]
+        sums = [psum.tile([P, S], F32, name=f"sums{u}") for u in range(len(units) - TILES)] + z
+        logs = [sb(f"logs{u}", [P, S], F32) for u in range(len(units))]
+        terms = [sb(f"terms{u}", [P, S], F32) for u in range(len(units))]
+        log_n = [sb(f"log_n{u}", [P, HALF], F32) for u in range(len(units))]
+        term_n = [sb(f"term_n{u}", [P, HALF], F32) for u in range(len(units))]
+
+        def turn(src, side, m):
+            for g in range(S // P):
+                col = side * HALF + (g % 2) * P
+                nc.tensor.transpose(turned[2 * m + g // 2][:, col : col + P], src[m][:, g * P : (g + 1) * P], ident[:])
+
+        scale_b(0)
+        turn(b, 1, 0)
         nc.vector.reciprocal(ra[0][:], ta[0][:])
-        nc.vector.tensor_scalar(rb500[:], rb300[:], 500.0 / 300.0, None, ALU.mult)
-        nc.vector.tensor_scalar(a[0][:], e[0][:], ra[0][:], 300.0, ALU.mult, ALU.mult)
+        scale_b(1)
+        scale_a(0)
+        turn(a, 0, 0)
+        turn(b, 1, 1)
         nc.vector.reciprocal(ra[1][:], ta[1][:])
-        nc.vector.scalar_tensor_tensor(s[0][:], lib_t[0][:], rb300[:, 0:1], a[0][:], ALU.mult, ALU.add)
-        nc.vector.tensor_scalar(a[1][:], e[1][:], ra[1][:], 300.0, ALU.mult, ALU.mult)
-        nc.vector.scalar_tensor_tensor(s[1][:], lib_t[1][:], rb300[:, 1:2], a[1][:], ALU.mult, ALU.add)
+        neg_sum(0)
+        scale_a(1)
+        turn(a, 0, 1)
+        neg_sum(1)
 
-        for m in range(TILES):
-            nc.scalar.activation(ln_a[m][:], a[m][:], ACT.Ln, scale=500.0 / 300.0, bias=0.01)
-            nc.scalar.activation(ln_m[m][:], s[m][:], ACT.Ln, scale=250.0 / 300.0, bias=0.01)
-            nc.scalar.activation(ln_b[m][:], lib_t[m][:], ACT.Ln, scale=rb500[:, m : m + 1], bias=0.01)
+        def cols(u):
+            return slice(units[u][1] * HALF, (units[u][1] + 1) * HALF)
 
-        def term_a(m):
-            nc.vector.tensor_tensor(t_a[m][:], a[m][:], ln_a[m][:], ALU.mult)
+        def multiply(u):
+            nc.vector.tensor_tensor(terms[u][:], turned[u][:], logs[u][:], ALU.mult)
+            for g in range(2):
+                for side in range(2):
+                    col = side * HALF + g * P
+                    nc.tensor.matmul(
+                        sums[u][:, g * P : (g + 1) * P], lhsT=terms[u][:, col : col + P], rhs=ident[:],
+                        start=(side == 0), stop=(side == 1), is_transpose=True,
+                    )
 
-        def term_m(m):
-            nc.vector.tensor_tensor(t_m[m][:], s[m][:], ln_m[m][:], ALU.mult)
+        def multiply_n(u):
+            nc.vector.tensor_tensor(term_n[u][:], n[units[u][0]][:, cols(u)], log_n[u][:], ALU.mult)
 
-        def term_b(m):
-            nc.vector.scalar_tensor_tensor(t_b[m][:], lib_t[m][:], rb300[:, m : m + 1], ln_b[m][:], ALU.mult, ALU.mult)
+        def finish(u):
+            m = units[u][0]
+            nc.vector.tensor_tensor(res[m][:, cols(u)], sums[u][:, :HALF], term_n[u][:], ALU.subtract)
+            nc.sync.dma_start(out=out[m * P : (m + 1) * P, cols(u)], in_=res[m][:, cols(u)])
 
-        def diff(m):
-            nc.vector.tensor_tensor(d[m][:], t_a[m][:], t_m[m][:], ALU.subtract)
-
-        def finish(m, cols):
-            nc.vector.tensor_tensor(res[m][:, cols], d[m][:, cols], t_b[m][:, cols], ALU.add)
-            nc.sync.dma_start(out=out[m * P : (m + 1) * P, cols], in_=res[m][:, cols])
-
-        term_a(0)
-        term_m(0)
-        term_b(0)
-        diff(0)
-        term_a(1)
-        finish(0, slice(0, S))
-        term_m(1)
-        term_b(1)
-        diff(1)
-        finish(1, slice(0, S // 2))
-        finish(1, slice(S // 2, S))
+        for u in range(len(units)):
+            nc.scalar.activation(logs[u][:], turned[u][:], ACT.Ln, scale=500.0 / 300.0, bias=0.01)
+        for u in range(len(units)):
+            nc.scalar.activation(log_n[u][:], n[units[u][0]][:, cols(u)], ACT.Ln, scale=250.0 / 300.0, bias=0.01)
+        for u in range(len(units)):
+            multiply(u)
+        for u in range(len(units) + 1):
+            if u < len(units):
+                multiply_n(u)
+            if u >= 1:
+                finish(u - 1)

@@ -156,12 +156,12 @@ def tile_picked_yspent_sim_p_kernel(tc, x_words, x_scales, hT, lib, offs, out):
         scale_b(0)
         turn(b, 1, 0)
         nc.vector.reciprocal(ra[0][:], ta[0][:])
-        scale_b(1)
         scale_a(0)
         turn(a, 0, 0)
+        scale_b(1)
         turn(b, 1, 1)
-        nc.vector.reciprocal(ra[1][:], ta[1][:])
         neg_sum(0)
+        nc.vector.reciprocal(ra[1][:], ta[1][:])
         scale_a(1)
         turn(a, 0, 1)
         neg_sum(1)
@@ -170,8 +170,13 @@ def tile_picked_yspent_sim_p_kernel(tc, x_words, x_scales, hT, lib, offs, out):
             return slice(units[u][1] * HALF, (units[u][1] + 1) * HALF)
 
         def multiply(u):
-            nc.vector.tensor_tensor(terms[u][:], turned[u][:], logs[u][:], ALU.mult)
+            last = u == len(units) - 1
+            if not last:
+                nc.vector.tensor_tensor(terms[u][:], turned[u][:], logs[u][:], ALU.mult)
             for g in range(2):
+                if last:
+                    views = [t[u][:].rearrange("p (s g c) -> p s g c", s=2, g=2)[:, :, g, :] for t in (terms, turned, logs)]
+                    nc.vector.tensor_tensor(*views, ALU.mult)
                 for side in range(2):
                     col = side * HALF + g * P
                     nc.tensor.matmul(
@@ -180,21 +185,37 @@ def tile_picked_yspent_sim_p_kernel(tc, x_words, x_scales, hT, lib, offs, out):
                     )
 
         def multiply_n(u):
-            nc.vector.tensor_tensor(term_n[u][:], n[units[u][0]][:, cols(u)], log_n[u][:], ALU.mult)
+            engine = nc.vector if u == len(units) - 1 else nc.gpsimd
+            engine.tensor_tensor(term_n[u][:], n[units[u][0]][:, cols(u)], log_n[u][:], ALU.mult)
 
         def finish(u):
             m = units[u][0]
             nc.vector.tensor_tensor(res[m][:, cols(u)], sums[u][:, :HALF], term_n[u][:], ALU.subtract)
             nc.sync.dma_start(out=out[m * P : (m + 1) * P, cols(u)], in_=res[m][:, cols(u)])
 
-        for u in range(len(units)):
+        def log_pair(u):
             nc.scalar.activation(logs[u][:], turned[u][:], ACT.Ln, scale=500.0 / 300.0, bias=0.01)
-        for u in range(len(units)):
+
+        def log_mean(u):
             nc.scalar.activation(log_n[u][:], n[units[u][0]][:, cols(u)], ACT.Ln, scale=250.0 / 300.0, bias=0.01)
-        for u in range(len(units)):
-            multiply(u)
-        for u in range(len(units) + 1):
-            if u < len(units):
-                multiply_n(u)
-            if u >= 1:
-                finish(u - 1)
+
+        log_pair(0)
+        log_mean(0)
+        log_pair(1)
+        log_mean(1)
+        log_pair(2)
+        log_pair(3)
+        log_mean(2)
+        log_mean(3)
+        multiply(0)
+        multiply_n(0)
+        multiply(1)
+        multiply_n(1)
+        finish(0)
+        multiply(2)
+        multiply(3)
+        multiply_n(2)
+        finish(1)
+        multiply_n(3)
+        finish(2)
+        finish(3)

from contextlib import ExitStack

import concourse.mybir as mybir
from concourse.masks import make_identity

K, T, S, V = 1024, 1024, 512, 256
FLOPS = 2 * K * V * S

F32 = mybir.dt.float32
BF16 = mybir.dt.bfloat16
I32 = mybir.dt.int32
U32 = mybir.dt.uint32
U16 = mybir.dt.uint16
U8 = mybir.dt.uint8
FP8X4 = mybir.dt.float8_e4m3fn_x4
ALU = mybir.AluOpType
ACT = mybir.ActivationFunctionType
AX = mybir.AxisListType

P = 128
PACK = 4
PASSES = K // (P * PACK)
TILES = V // P


def tile_picked_yspent_sim_p_kernel(tc, x_words, x_scales, hT, lib, offs, out):
    nc = tc.nc
    with ExitStack() as ctx:
        keep = ctx.enter_context(tc.tile_pool(name="keep", bufs=1))
        psum = ctx.enter_context(tc.psum_pool(name="psum", bufs=1))

        def sb(name, shape, dtype):
            return keep.tile(shape, dtype, name=name, align_bytes=64)

        offsets = keep.tile([P, S // 16], U16, name="offsets")
        nc.sync.dma_start(offsets[:], offs)

        x_planes = sb("x_planes", [P, T], U8)
        nc.vector.memset(x_planes[:].bitcast(I32), 0)
        warm = sb("warm", [P, 2], F32)
        nc.vector.memset(warm[:, 0:1], 0.0)
        ident = sb("ident", [P, P], F32)
        make_identity(nc, ident[:])
        nc.scalar.activation(warm[:, 1:2], warm[:, 0:1], ACT.Exp)

        x_table, h_raw = [], []
        for o in range(PASSES):
            xt = sb(f"x_table{o}", [P, T], I32)
            nc.sync.dma_start(out=xt[:], in_=x_words[o].rearrange("p c r -> p (c r)").bitcast(I32))
            x_table.append(xt)
            if o == 0:
                for q in range(4):
                    nc.sync.dma_start(
                        out=x_planes[32 * q : 32 * q + 4 * PASSES, :].bitcast(I32),
                        in_=x_scales[:, 4 * q : 4 * q + 4, :].bitcast(I32),
                    )
            hr = sb(f"h_raw{o}", [P, PACK, V], F32)
            nc.sync.dma_start(out=hr[:], in_=hT[o * P * PACK : (o + 1) * P * PACK, :].rearrange("(p j) v -> p j v", j=PACK))
            h_raw.append(hr)
        lib_t = []
        for m in range(TILES):
            lt = sb(f"lib{m}", [P, S], F32)
            nc.sync.dma_start(out=lt[:], in_=lib[m * P : (m + 1) * P, :])
            lib_t.append(lt)

        x_codes = [sb(f"x_codes{o}", [P, S], U32) for o in range(PASSES)]
        x_sc = sb("x_sc", [P, S], U8)
        h_bf = [[sb(f"h_bf{o}{m}", [P, P, PACK], BF16) for m in range(TILES)] for o in range(PASSES)]
        h_codes = [[sb(f"h_codes{o}{m}", [P, P], U32) for m in range(TILES)] for o in range(PASSES)]
        h_sc = [[sb(f"h_sc{o}{m}", [P, P], U8) for m in range(TILES)] for o in range(PASSES)]
        z = [psum.tile([P, S], F32, name=f"z{m}") for m in range(TILES)]

        def gather_words(o):
            nc.vector.tensor_copy(x_codes[o][:], x_table[o][:].bitcast(U32).indirect(offsets[:]))

        def weave(copy, o, m):
            copy(
                h_bf[o][m][:].rearrange("p (c i) j -> p c j i", i=4),
                h_raw[o][:, :, m * P : (m + 1) * P].rearrange("p j (c i) -> p c j i", i=4),
            )

        def quantise(o, m):
            nc.vector.quantize_mx(
                out=h_codes[o][m][:].bitcast(FP8X4),
                scales=h_sc[o][m][:],
                in_=h_bf[o][m][:].rearrange("p c j -> p (c j)"),
            )

        def product(o, m):
            nc.tensor.matmul_mx(
                out=z[m][:],
                lhsT=h_codes[o][m][:].bitcast(FP8X4),
                lhsT_scale=h_sc[o][m][:],
                rhs=x_codes[o][:].bitcast(FP8X4),
                rhs_scale=x_sc[4 * o :, :],
                start=(o == 0),
                stop=(o == PASSES - 1),
            )

        gather_words(0)
        nc.vector.tensor_copy(x_sc[:], x_planes[:].indirect(offsets[:]))
        weave(nc.scalar.copy, 0, 0)
        weave(nc.scalar.copy, 0, 1)
        quantise(0, 0)
        quantise(0, 1)
        product(0, 0)
        product(0, 1)
        gather_words(1)
        weave(nc.scalar.copy, 1, 0)
        weave(nc.vector.tensor_copy, 1, 1)
        quantise(1, 0)
        quantise(1, 1)
        product(1, 0)
        product(1, 1)

        neg_max = [sb(f"neg_max{m}", [P, 1], F32) for m in range(TILES)]
        ta = [sb(f"ta{m}", [P, 1], F32) for m in range(TILES)]
        ra = [sb(f"ra{m}", [P, 1], F32) for m in range(TILES)]
        tb = sb("tb", [P, TILES], F32)
        rb = sb("rb", [P, TILES], F32)
        e = [sb(f"e{m}", [P, S], F32) for m in range(TILES)]
        a = [sb(f"a{m}", [P, S], F32) for m in range(TILES)]
        b = [sb(f"b{m}", [P, S], F32) for m in range(TILES)]
        n = [sb(f"n{m}", [P, S], F32) for m in range(TILES)]
        res = [sb(f"res{m}", [P, S], F32) for m in range(TILES)]

        for m in range(TILES):
            nc.scalar.activation(e[m][:], lib_t[m][:], ACT.Copy, scale=1.0 / 300.0, accum_out=tb[:, m : m + 1])
        for m in range(TILES):
            nc.vector.tensor_reduce(neg_max[m][:], z[m][:], AX.X, ALU.max, negate=True)
            nc.scalar.activation(e[m][:], z[m][:], ACT.Exp, bias=neg_max[m][:], accum_out=ta[m][:])
        nc.vector.reciprocal(rb[:], tb[:])
        def scale_b(m):
            nc.vector.tensor_scalar(b[m][:], lib_t[m][:], rb[:, m : m + 1], None, ALU.mult)

        def scale_a(m):
            nc.vector.tensor_scalar(a[m][:], e[m][:], ra[m][:], 300.0, ALU.mult, ALU.mult)

        def neg_sum(m):
            nc.vector.tensor_tensor(n[m][:], a[m][:], b[m][:], ALU.add)

        HALF = S // 2
        units = [(m, h) for m in range(TILES) for h in range(2)]
        turned = [psum.tile([P, S], F32, name=f"turned{u}") for u in range(len(units))]
        sums = [psum.tile([P, S], F32, name=f"sums{u}") for u in range(len(units) - TILES)] + z
        logs = [sb(f"logs{u}", [P, S], F32) for u in range(len(units))]
        terms = [sb(f"terms{u}", [P, S], F32) for u in range(len(units))]
        log_n = [sb(f"log_n{u}", [P, HALF], F32) for u in range(len(units))]
        term_n = [sb(f"term_n{u}", [P, HALF], F32) for u in range(len(units))]

        def turn(src, side, m):
            for g in range(S // P):
                col = side * HALF + (g % 2) * P
                nc.tensor.transpose(turned[2 * m + g // 2][:, col : col + P], src[m][:, g * P : (g + 1) * P], ident[:])

        scale_b(0)
        turn(b, 1, 0)
        nc.vector.reciprocal(ra[0][:], ta[0][:])
        scale_a(0)
        turn(a, 0, 0)
        scale_b(1)
        turn(b, 1, 1)
        neg_sum(0)
        nc.vector.reciprocal(ra[1][:], ta[1][:])
        scale_a(1)
        turn(a, 0, 1)
        neg_sum(1)

        def cols(u):
            return slice(units[u][1] * HALF, (units[u][1] + 1) * HALF)

        def multiply(u):
            last = u == len(units) - 1
            if not last:
                nc.vector.tensor_tensor(terms[u][:], turned[u][:], logs[u][:], ALU.mult)
            for g in range(2):
                if last:
                    views = [t[u][:].rearrange("p (s g c) -> p s g c", s=2, g=2)[:, :, g, :] for t in (terms, turned, logs)]
                    nc.vector.tensor_tensor(*views, ALU.mult)
                for side in range(2):
                    col = side * HALF + g * P
                    nc.tensor.matmul(
                        sums[u][:, g * P : (g + 1) * P], lhsT=terms[u][:, col : col + P], rhs=ident[:],
                        start=(side == 0), stop=(side == 1), is_transpose=True,
                    )

        def multiply_n(u):
            engine = nc.vector if u == len(units) - 1 else nc.gpsimd
            engine.tensor_tensor(term_n[u][:], n[units[u][0]][:, cols(u)], log_n[u][:], ALU.mult)

        def finish(u):
            m = units[u][0]
            nc.vector.tensor_tensor(res[m][:, cols(u)], sums[u][:, :HALF], term_n[u][:], ALU.subtract)
            nc.sync.dma_start(out=out[m * P : (m + 1) * P, cols(u)], in_=res[m][:, cols(u)])

        def log_pair(u):
            nc.scalar.activation(logs[u][:], turned[u][:], ACT.Ln, scale=500.0 / 300.0, bias=0.01)

        def log_mean(u):
            nc.scalar.activation(log_n[u][:], n[units[u][0]][:, cols(u)], ACT.Ln, scale=250.0 / 300.0, bias=0.01)

        log_pair(0)
        log_mean(0)
        log_pair(1)
        log_mean(1)
        log_pair(2)
        log_pair(3)
        log_mean(2)
        log_mean(3)
        multiply(0)
        multiply_n(0)
        multiply(1)
        multiply_n(1)
        finish(0)
        multiply(2)
        multiply(3)
        multiply_n(2)
        finish(1)
        multiply_n(3)
        finish(2)
        finish(3)
